import numpy as np, ml_dtypes
CORES = [24,26,29,31,48,50,53,55]
N = 8
TK = 128
def setup_inputs(rng):
    rt = (0.75 * rng.standard_normal((128, 1), dtype=np.float32) + rng.standard_normal((128, N), dtype=np.float32) / 2).astype(ml_dtypes.bfloat16)
    return {"x": rng.standard_normal((N, 128, TK), dtype=np.float32).astype(ml_dtypes.bfloat16), "rt": np.broadcast_to(rt, (N, 128, N)).copy(), "w": rng.standard_normal((N, 128, 128), dtype=np.float32).astype(ml_dtypes.bfloat16)}
def setup_inputs_big(rng):
    d = setup_inputs(rng)
    for k in ("x", "w"): d[k] = (d[k].astype(np.float32) * 1024.0).astype(d[k].dtype)
    return d
def setup_inputs_small(rng):
    d = setup_inputs(rng)
    for k in ("x", "w"): d[k] = (d[k].astype(np.float32) * (1 / 1024.0)).astype(d[k].dtype)
    return d
def reference(x, rt, w):
    X, RT, W = x.astype(np.float64), rt.astype(np.float64), w.astype(np.float64)
    y = np.zeros((N, 128, TK))
    for r in range(N):
        sc = RT[r].T @ X[r]
        g = np.exp(sc - sc.max(axis=0)); g = g / g.sum(axis=0)
        y[r] = sum(g[j] * (W[j].T @ X[r]) for j in range(N))
    return {"y": y.astype(ml_dtypes.bfloat16)}

@@ -1,0 +1,194 @@
+from concourse.bass import DstId, RemoteDMATransfer
+from concourse.mybir import AluOpType, AxisListType, ActivationFunctionType
+
+N = 8
+D = 128
+
+SCRATCH = {
+    "wall": ("sbuf", [128, N * D], "bfloat16"),
+    "xs": ("sbuf", [128, D], "bfloat16"),
+    "rts": ("sbuf", [128, N], "bfloat16"),
+    "pmi": ("sbuf", [128, D], "bfloat16"),
+    "ident": ("sbuf", [128, D], "bfloat16"),
+    "xts": ("sbuf", [128, D], "bfloat16"),
+    "negm": ("sbuf", [128, 4], "float32"),
+    "ee": ("sbuf", [128, N], "float32"),
+    "ssum": ("sbuf", [128, 4], "float32"),
+    "rs": ("sbuf", [128, 4], "float32"),
+    "dg": ("sbuf", [128, N * D], "bfloat16"),
+    "xg": ("sbuf", [128, N * D], "bfloat16"),
+    "ysb": ("sbuf", [128, D], "bfloat16"),
+    "st_ps": ("psum", [128, 512], "float32"),
+    "xt_ps": ("psum", [128, 1024], "bfloat16"),
+    "xg_ps0": ("psum", [128, 512], "float32"),
+    "xg_ps1": ("psum", [128, 512], "float32"),
+    "xg_ps2": ("psum", [128, 512], "float32"),
+    "xg_ps3": ("psum", [128, 512], "float32"),
+    "y_ps": ("psum", [128, 512], "float32"),
+}
+SEMAPHORES = ["ld_w", "ld_x", "ld_rt", "s_io", "s_id", "s_st", "s_xt", "s_xts", "s_nm", "s_e", "s_rs",
+              "s_d0", "s_d1", "s_d2", "s_d3", "s_m0", "s_m1", "s_m2", "s_m3", "s_c0", "s_c1", "s_c2", "s_c3",
+              "a_q", "a_p", "a_fd", "a_rl", "a_fw", "sent", "s_y", "s_yc", "st_y"]
+
+
+def _bits(mask):
+    return [b for b in range(16) if (mask >> b) & 1]
+
+
+def rank_program(g, core, T, topo):
+    if T.rank_of(core) is None:
+        return
+    S = T.sem
+    cores = list(T.cores)
+
+    def near_of(c):
+        return [d for d in cores if d != c and topo.chip(d) == topo.chip(c)]
+
+    def far_of(c):
+        return [d for d in cores if topo.chip(d) != topo.chip(c)]
+
+    def is_port(c):
+        return all(topo.may_write(c, d) for d in far_of(c))
+
+    def partner(p):
+        return [q for q in far_of(p) if not is_port(q) and topo.die(q) == topo.die(p)][0]
+
+    chips = []
+    for c in cores:
+        if topo.chip(c) not in chips:
+            chips.append(topo.chip(c))
+    order = []
+    for ch in chips:
+        mine = [c for c in cores if topo.chip(c) == ch]
+        order += [c for c in mine if not is_port(c)] + [c for c in mine if is_port(c)]
+    slot = {c: s for s, c in enumerate(order)}
+
+    def W(c0, c1=None):
+        c1 = c0 if c1 is None else c1
+        return T.wall[:, slot[c0] * D:(slot[c1] + 1) * D]
+
+    def send(pieces):
+        trs = []
+        n = 0
+        for ap, dsts, mask, sem in pieces:
+            ids = []
+            for d in dsts:
+                a = topo.addr(d)
+                ids.append(DstId(rid=a[0], pnc=a[1]))
+            trs.append(RemoteDMATransfer(dst_ids=ids, dma_engine_mask=mask, remote_sem=sem,
+                                         srcs=[ap], dsts=[ap for d in dsts], alu_op=0))
+            n += len(_bits(mask))
+        g.remote_dma_fused(trs, local_sem=S.sent)
+        return n
+
+    near, far = near_of(core), far_of(core)
+    port = is_port(core)
+    near_q = [c for c in near if not is_port(c)]
+    near_p = [c for c in near if is_port(c)]
+    far_q = [c for c in far if not is_port(c)]
+    far_p = [c for c in far if is_port(c)]
+    m_on = topo.mask(core, near[0])
+    n_on = len(_bits(m_on))
+    n_off = len(_bits(topo.mask(far_p[0], core)))
+    n_rest = n_on - n_off
+
+    g.sync.dma_start(W(core), T.w[:, :]).then_inc(S.ld_w, 16)
+    g.scalar.dma_start(T.xs[:, :], T.x[:, :]).then_inc(S.ld_x, 16)
+    g.sync.dma_start(T.rts[:, :], T.rt[:, :]).then_inc(S.ld_rt, 16)
+
+    g.iota(T.pmi[:, :], [[-1, D]], 0, 1, allow_small_or_imprecise_dtypes=True).then_inc(S.s_io, 1)
+    g.wait_ge(S.ld_w, 16)
+    sent = 0
+    src = None
+    if port:
+        m_off = topo.mask(core, far[0])
+        sent += send([(W(core), [partner(core)], m_off, S.a_fd),
+                      (W(core), near, m_on & ~m_off, S.a_p)])
+        g.wait_ge(S.a_q, n_on * len(near_q))
+        mine = [d for d in far if topo.die(d) == topo.die(core)]
+        sent += send([(W(near_q[0], near_q[-1]), mine, m_off, S.a_fw)])
+    else:
+        sent += send([(W(core), near_p, m_on, S.a_q)])
+        sent += send([(W(core), near_q, m_on, S.a_q)])
+        src = [p for p in far_p if partner(p) == core][0]
+        g.wait_ge(S.a_fd, n_off)
+        sent += send([(W(src), near, m_on, S.a_rl)])
+    g.wait_ge(S.sent, sent)
+
+    arrivals = [(S.ld_w, 16, [core]), (S.a_q, n_on * len(near_q), near_q), (S.a_p, n_rest * len(near_p), near_p)]
+    if port:
+        arrivals.append((S.a_rl, n_on * len(far_p), far_p))
+    else:
+        arrivals.append((S.a_fd, n_off, [src]))
+        arrivals.append((S.a_rl, n_on * (len(far_p) - 1), [p for p in far_p if p != src]))
+    arrivals.append((S.a_fw, n_off, far_q))
+
+    ci = chips.index(topo.chip(core))
+    pairs = [2 * ci, 2 * ci + 1, 2 * (1 - ci) + 1, 2 * (1 - ci)]
+    ps = [T.xg_ps0, T.xg_ps1, T.xg_ps2, T.xg_ps3]
+    s_d = [S.s_d0, S.s_d1, S.s_d2, S.s_d3]
+    s_m = [S.s_m0, S.s_m1, S.s_m2, S.s_m3]
+    s_c = [S.s_c0, S.s_c1, S.s_c2, S.s_c3]
+
+    pe = g.tensor
+    pe.wait_ge(S.ld_x, 16)
+    pe.wait_ge(S.ld_rt, 16)
+    pe.matmul(T.st_ps[:, 0:N], T.xs[:, :], T.rts[:, :], start=True, stop=True).then_inc(S.s_st, 1)
+    pe.wait_ge(S.s_id, 1)
+    pe.transpose(T.xt_ps[:, 0:D], T.xs[:, :], T.ident[:, :]).then_inc(S.s_xt, 1)
+    pe.wait_ge(S.s_xts, 1)
+    for i, h in enumerate(pairs):
+        pe.wait_ge(s_d[i], 2)
+        pe.matmul(ps[i][:, 0:2 * D], T.xts[:, :], T.dg[:, h * 2 * D:(h + 1) * 2 * D],
+                  start=True, stop=True).then_inc(s_m[i], 1)
+    seq = [(sem, cnt, c) for sem, cnt, cs in arrivals for c in cs]
+    waited = []
+    mm = None
+    for k, (sem, cnt, c) in enumerate(seq):
+        i = pairs.index(slot[c] // 2)
+        if i not in waited:
+            pe.wait_ge(s_c[i], 1)
+            waited.append(i)
+        pe.wait_ge(sem, cnt)
+        mm = pe.matmul(T.y_ps[:, 0:D], W(c), T.xg[:, slot[c] * D:(slot[c] + 1) * D],
+                       start=(k == 0), stop=(k == len(seq) - 1))
+    mm.then_inc(S.s_y, 1)
+
+    act = g.scalar
+    act.wait_ge(S.s_nm, 1)
+    act.activation(T.ee[:, :], T.st_ps[:, 0:N], ActivationFunctionType.Exp, bias=T.negm[:, 0:1], scale=1.0,
+                   accum_out=T.ssum[:, 0:1]).then_inc(S.s_e, 1)
+    for i in (0, 2):
+        h = pairs[i]
+        act.wait_ge(s_m[i], 1)
+        act.activation(T.xg[:, h * 2 * D:(h + 1) * 2 * D], ps[i][:, 0:2 * D],
+                       ActivationFunctionType.Copy).then_inc(s_c[i], 1)
+
+    ve = g.vector
+    ve.wait_ge(S.s_io, 1)
+    ve.tensor_scalar(out=T.ident[:, :], in0=T.pmi[:, :], scalar1=0.0, scalar2=None,
+                     op0=AluOpType.is_equal).then_inc(S.s_id, 1)
+    ve.wait_ge(S.s_st, 1)
+    ve.tensor_reduce(out=T.negm[:, 0:1], in_=T.st_ps[:, 0:N], axis=AxisListType.X, op=AluOpType.max,
+                     negate=True).then_inc(S.s_nm, 1)
+    ve.wait_ge(S.s_xt, 1)
+    ve.tensor_copy(T.xts[:, :], T.xt_ps[:, 0:D]).then_inc(S.s_xts, 1)
+    ve.wait_ge(S.s_e, 1)
+    ve.reciprocal(T.rs[:, 0:1], T.ssum[:, 0:1]).then_inc(S.s_rs, 1)
+    ve.wait_ge(S.s_rs, 1)
+    ve.wait_ge(S.s_id, 1)
+    for i, h in enumerate(pairs):
+        for s in (2 * h, 2 * h + 1):
+            j = T.rank_of(order[s])
+            ve.tensor_scalar(out=T.dg[:, s * D:(s + 1) * D], in0=T.ident[:, :], scalar1=T.ee[:, j:j + 1],
+                             scalar2=T.rs[:, 0:1], op0=AluOpType.mult, op1=AluOpType.mult).then_inc(s_d[i], 1)
+    for i in (1, 3):
+        h = pairs[i]
+        ve.wait_ge(s_m[i], 1)
+        ve.tensor_copy(T.xg[:, h * 2 * D:(h + 1) * 2 * D], ps[i][:, 0:2 * D]).then_inc(s_c[i], 1)
+    ve.wait_ge(S.s_y, 1)
+    ve.tensor_copy(T.ysb[:, :], T.y_ps[:, 0:D]).then_inc(S.s_yc, 1)
+
+    g.sync.wait_ge(S.s_yc, 1)
+    g.sync.dma_start(T.y[:, :], T.ysb[:, :]).then_inc(S.st_y, 16)
+    g.sync.wait_ge(S.st_y, 16)

@@ -3,12 +3,14 @@ from concourse.mybir import AluOpType, AxisListType, ActivationFunctionType
 
 N = 8
 D = 128
+H = D // 2
 
 SCRATCH = {
     "wall": ("sbuf", [128, N * D], "bfloat16"),
     "xs": ("sbuf", [128, D], "bfloat16"),
     "rts": ("sbuf", [128, N], "bfloat16"),
     "pmi": ("sbuf", [128, D], "bfloat16"),
+    "sq": ("sbuf", [128, D], "float32"),
     "ident": ("sbuf", [128, D], "bfloat16"),
     "xts": ("sbuf", [128, D], "bfloat16"),
     "negm": ("sbuf", [128, 4], "float32"),
@@ -26,9 +28,9 @@ SCRATCH = {
     "xg_ps3": ("psum", [128, 512], "float32"),
     "y_ps": ("psum", [128, 512], "float32"),
 }
-SEMAPHORES = ["ld_w", "ld_x", "ld_rt", "s_io", "s_id", "s_st", "s_xt", "s_xts", "s_nm", "s_e", "s_rs",
+SEMAPHORES = ["ld_w", "ld_x", "ld_rt", "s_io", "a_io", "s_sq", "s_id", "s_st", "s_xt", "s_xts", "s_nm", "s_e", "s_rs",
               "s_d0", "s_d1", "s_d2", "s_d3", "s_m0", "s_m1", "s_m2", "s_m3", "s_c0", "s_c1", "s_c2", "s_c3",
-              "a_q", "a_p", "a_fd", "a_rl", "a_fw", "sent", "s_y", "s_yc", "st_y"]
+              "a_h", "a_q", "a_p", "a_fd", "a_rl", "a_fw", "a_r2", "sent", "s_y", "s_yc", "st_y"]
 
 
 def _bits(mask):
@@ -63,9 +65,8 @@ def rank_program(g, core, T, topo):
         order += [c for c in mine if not is_port(c)] + [c for c in mine if is_port(c)]
     slot = {c: s for s, c in enumerate(order)}
 
-    def W(c0, c1=None):
-        c1 = c0 if c1 is None else c1
-        return T.wall[:, slot[c0] * D:(slot[c1] + 1) * D]
+    def W(c):
+        return T.wall[:, slot[c] * D:(slot[c] + 1) * D]
 
     def send(pieces):
         trs = []
@@ -87,6 +88,7 @@ def rank_program(g, core, T, topo):
     near_p = [c for c in near if is_port(c)]
     far_q = [c for c in far if not is_port(c)]
     far_p = [c for c in far if is_port(c)]
+    buddy = [c for c in near if topo.die(c) == topo.die(core)][0]
     m_on = topo.mask(core, near[0])
     n_on = len(_bits(m_on))
     n_off = len(_bits(topo.mask(far_p[0], core)))
@@ -96,32 +98,43 @@ def rank_program(g, core, T, topo):
     g.scalar.dma_start(T.xs[:, :], T.x[:, :]).then_inc(S.ld_x, 16)
     g.sync.dma_start(T.rts[:, :], T.rt[:, :]).then_inc(S.ld_rt, 16)
 
-    g.iota(T.pmi[:, :], [[-1, D]], 0, 1, allow_small_or_imprecise_dtypes=True).then_inc(S.s_io, 1)
+    o0 = H if port else 0
+    b0 = H - o0
+    g.iota(T.pmi[:, o0:o0 + H], [[-1, H]], -o0, 1, allow_small_or_imprecise_dtypes=True).then_inc(S.s_io, 1)
+    g.wait_ge(S.s_io, 1)
+    sent = send([(T.pmi[:, o0:o0 + H], [buddy], m_on, S.a_io)])
     g.wait_ge(S.ld_w, 16)
-    sent = 0
-    src = None
     if port:
         m_off = topo.mask(core, far[0])
         sent += send([(W(core), [partner(core)], m_off, S.a_fd),
                       (W(core), near, m_on & ~m_off, S.a_p)])
-        g.wait_ge(S.a_q, n_on * len(near_q))
-        mine = [d for d in far if topo.die(d) == topo.die(core)]
-        sent += send([(W(near_q[0], near_q[-1]), mine, m_off, S.a_fw)])
+        g.wait_ge(S.a_h, n_on)
+        sent += send([(W(buddy), [f for f in far_p if topo.die(f) == topo.die(core)], m_off, S.a_fw)])
+        src = [q for q in far_q if topo.die(q) == topo.die(core)][0]
+        g.wait_ge(S.a_fw, n_off)
+        sent += send([(W(src), near, m_on, S.a_r2)])
     else:
-        sent += send([(W(core), near_p, m_on, S.a_q)])
-        sent += send([(W(core), near_q, m_on, S.a_q)])
+        sent += send([(W(core), [buddy], m_on, S.a_h)])
+        sent += send([(W(core), [c for c in near if c != buddy], m_on, S.a_q)])
         src = [p for p in far_p if partner(p) == core][0]
         g.wait_ge(S.a_fd, n_off)
         sent += send([(W(src), near, m_on, S.a_rl)])
     g.wait_ge(S.sent, sent)
 
-    arrivals = [(S.ld_w, 16, [core]), (S.a_q, n_on * len(near_q), near_q), (S.a_p, n_rest * len(near_p), near_p)]
+    arrivals = [(S.ld_w, 16, [core])]
     if port:
+        arrivals.append((S.a_h, n_on, [buddy]))
+        arrivals.append((S.a_q, n_on, [q for q in near_q if q != buddy]))
+        arrivals.append((S.a_p, n_rest * len(near_p), near_p))
         arrivals.append((S.a_rl, n_on * len(far_p), far_p))
+        arrivals.append((S.a_fw, n_off, [src]))
+        arrivals.append((S.a_r2, n_on * (len(far_q) - 1), [q for q in far_q if q != src]))
     else:
+        arrivals.append((S.a_q, n_on * len(near_q), near_q))
+        arrivals.append((S.a_p, n_rest * len(near_p), near_p))
         arrivals.append((S.a_fd, n_off, [src]))
         arrivals.append((S.a_rl, n_on * (len(far_p) - 1), [p for p in far_p if p != src]))
-    arrivals.append((S.a_fw, n_off, far_q))
+        arrivals.append((S.a_r2, n_on * len(far_q), far_q))
 
     ci = chips.index(topo.chip(core))
     pairs = [2 * ci, 2 * ci + 1, 2 * (1 - ci) + 1, 2 * (1 - ci)]
@@ -134,7 +147,7 @@ def rank_program(g, core, T, topo):
     pe.wait_ge(S.ld_x, 16)
     pe.wait_ge(S.ld_rt, 16)
     pe.matmul(T.st_ps[:, 0:N], T.xs[:, :], T.rts[:, :], start=True, stop=True).then_inc(S.s_st, 1)
-    pe.wait_ge(S.s_id, 1)
+    pe.wait_ge(S.s_id, 2)
     pe.transpose(T.xt_ps[:, 0:D], T.xs[:, :], T.ident[:, :]).then_inc(S.s_xt, 1)
     pe.wait_ge(S.s_xts, 1)
     for i, h in enumerate(pairs):
@@ -155,6 +168,12 @@ def rank_program(g, core, T, topo):
     mm.then_inc(S.s_y, 1)
 
     act = g.scalar
+    for n_done, (c0, sem, cnt) in enumerate(((o0, S.s_io, 1), (b0, S.a_io, n_on))):
+        act.wait_ge(sem, cnt)
+        act.activation(T.sq[:, c0:c0 + H], T.pmi[:, c0:c0 + H], ActivationFunctionType.Square).then_inc(S.s_sq, 1)
+        act.wait_ge(S.s_sq, n_done + 1)
+        act.activation(T.ident[:, c0:c0 + H], T.sq[:, c0:c0 + H], ActivationFunctionType.Exp,
+                       scale=-100.0).then_inc(S.s_id, 1)
     act.wait_ge(S.s_nm, 1)
     act.activation(T.ee[:, :], T.st_ps[:, 0:N], ActivationFunctionType.Exp, bias=T.negm[:, 0:1], scale=1.0,
                    accum_out=T.ssum[:, 0:1]).then_inc(S.s_e, 1)
@@ -165,18 +184,15 @@ def rank_program(g, core, T, topo):
                        ActivationFunctionType.Copy).then_inc(s_c[i], 1)
 
     ve = g.vector
-    ve.wait_ge(S.s_io, 1)
-    ve.tensor_scalar(out=T.ident[:, :], in0=T.pmi[:, :], scalar1=0.0, scalar2=None,
-                     op0=AluOpType.is_equal).then_inc(S.s_id, 1)
     ve.wait_ge(S.s_st, 1)
     ve.tensor_reduce(out=T.negm[:, 0:1], in_=T.st_ps[:, 0:N], axis=AxisListType.X, op=AluOpType.max,
                      negate=True).then_inc(S.s_nm, 1)
-    ve.wait_ge(S.s_xt, 1)
-    ve.tensor_copy(T.xts[:, :], T.xt_ps[:, 0:D]).then_inc(S.s_xts, 1)
     ve.wait_ge(S.s_e, 1)
     ve.reciprocal(T.rs[:, 0:1], T.ssum[:, 0:1]).then_inc(S.s_rs, 1)
+    ve.wait_ge(S.s_xt, 1)
+    ve.tensor_copy(T.xts[:, :], T.xt_ps[:, 0:D]).then_inc(S.s_xts, 1)
     ve.wait_ge(S.s_rs, 1)
-    ve.wait_ge(S.s_id, 1)
+    ve.wait_ge(S.s_id, 2)
     for i, h in enumerate(pairs):
         for s in (2 * h, 2 * h + 1):
             j = T.rank_of(order[s])

from concourse.bass import DstId, RemoteDMATransfer
from concourse.mybir import AluOpType, AxisListType, ActivationFunctionType

N = 8
D = 128
H = D // 2

SCRATCH = {
    "wall": ("sbuf", [128, N * D], "bfloat16"),
    "xs": ("sbuf", [128, D], "bfloat16"),
    "rts": ("sbuf", [128, N], "bfloat16"),
    "pmi": ("sbuf", [128, D], "bfloat16"),
    "sq": ("sbuf", [128, D], "float32"),
    "ident": ("sbuf", [128, D], "bfloat16"),
    "xts": ("sbuf", [128, D], "bfloat16"),
    "negm": ("sbuf", [128, 4], "float32"),
    "ee": ("sbuf", [128, N], "float32"),
    "ssum": ("sbuf", [128, 4], "float32"),
    "rs": ("sbuf", [128, 4], "float32"),
    "dg": ("sbuf", [128, N * D], "bfloat16"),
    "xg": ("sbuf", [128, N * D], "bfloat16"),
    "ysb": ("sbuf", [128, D], "bfloat16"),
    "st_ps": ("psum", [128, 512], "float32"),
    "xt_ps": ("psum", [128, 1024], "bfloat16"),
    "xg_ps0": ("psum", [128, 512], "float32"),
    "xg_ps1": ("psum", [128, 512], "float32"),
    "xg_ps2": ("psum", [128, 512], "float32"),
    "xg_ps3": ("psum", [128, 512], "float32"),
    "y_ps": ("psum", [128, 512], "float32"),
}
SEMAPHORES = ["ld_w", "ld_x", "ld_rt", "s_io", "a_io", "s_sq", "s_id", "s_st", "s_xt", "s_xts", "s_nm", "s_e", "s_rs",
              "s_d0", "s_d1", "s_d2", "s_d3", "s_m0", "s_m1", "s_m2", "s_m3", "s_c0", "s_c1", "s_c2", "s_c3",
              "a_h", "a_q", "a_p", "a_fd", "a_rl", "a_fw", "a_r2", "sent", "s_y", "s_yc", "st_y"]


def _bits(mask):
    return [b for b in range(16) if (mask >> b) & 1]


def rank_program(g, core, T, topo):
    if T.rank_of(core) is None:
        return
    S = T.sem
    cores = list(T.cores)

    def near_of(c):
        return [d for d in cores if d != c and topo.chip(d) == topo.chip(c)]

    def far_of(c):
        return [d for d in cores if topo.chip(d) != topo.chip(c)]

    def is_port(c):
        return all(topo.may_write(c, d) for d in far_of(c))

    def partner(p):
        return [q for q in far_of(p) if not is_port(q) and topo.die(q) == topo.die(p)][0]

    chips = []
    for c in cores:
        if topo.chip(c) not in chips:
            chips.append(topo.chip(c))
    order = []
    for ch in chips:
        mine = [c for c in cores if topo.chip(c) == ch]
        order += [c for c in mine if not is_port(c)] + [c for c in mine if is_port(c)]
    slot = {c: s for s, c in enumerate(order)}

    def W(c):
        return T.wall[:, slot[c] * D:(slot[c] + 1) * D]

    def send(pieces):
        trs = []
        n = 0
        for ap, dsts, mask, sem in pieces:
            ids = []
            for d in dsts:
                a = topo.addr(d)
                ids.append(DstId(rid=a[0], pnc=a[1]))
            trs.append(RemoteDMATransfer(dst_ids=ids, dma_engine_mask=mask, remote_sem=sem,
                                         srcs=[ap], dsts=[ap for d in dsts], alu_op=0))
            n += len(_bits(mask))
        g.remote_dma_fused(trs, local_sem=S.sent)
        return n

    near, far = near_of(core), far_of(core)
    port = is_port(core)
    near_q = [c for c in near if not is_port(c)]
    near_p = [c for c in near if is_port(c)]
    far_q = [c for c in far if not is_port(c)]
    far_p = [c for c in far if is_port(c)]
    buddy = [c for c in near if topo.die(c) == topo.die(core)][0]
    m_on = topo.mask(core, near[0])
    n_on = len(_bits(m_on))
    n_off = len(_bits(topo.mask(far_p[0], core)))
    n_rest = n_on - n_off

    g.sync.dma_start(W(core), T.w[:, :]).then_inc(S.ld_w, 16)
    g.scalar.dma_start(T.xs[:, :], T.x[:, :]).then_inc(S.ld_x, 16)
    g.sync.dma_start(T.rts[:, :], T.rt[:, :]).then_inc(S.ld_rt, 16)

    o0 = H if port else 0
    b0 = H - o0
    g.iota(T.pmi[:, o0:o0 + H], [[-1, H]], -o0, 1, allow_small_or_imprecise_dtypes=True).then_inc(S.s_io, 1)
    g.wait_ge(S.s_io, 1)
    sent = send([(T.pmi[:, o0:o0 + H], [buddy], m_on, S.a_io)])
    g.wait_ge(S.ld_w, 16)
    if port:
        m_off = topo.mask(core, far[0])
        sent += send([(W(core), [partner(core)], m_off, S.a_fd),
                      (W(core), near, m_on & ~m_off, S.a_p)])
        g.wait_ge(S.a_h, n_on)
        sent += send([(W(buddy), [f for f in far_p if topo.die(f) == topo.die(core)], m_off, S.a_fw)])
        src = [q for q in far_q if topo.die(q) == topo.die(core)][0]
        g.wait_ge(S.a_fw, n_off)
        sent += send([(W(src), near, m_on, S.a_r2)])
    else:
        sent += send([(W(core), [buddy], m_on, S.a_h)])
        sent += send([(W(core), [c for c in near if c != buddy], m_on, S.a_q)])
        src = [p for p in far_p if partner(p) == core][0]
        g.wait_ge(S.a_fd, n_off)
        sent += send([(W(src), near, m_on, S.a_rl)])
    g.wait_ge(S.sent, sent)

    arrivals = [(S.ld_w, 16, [core])]
    if port:
        arrivals.append((S.a_h, n_on, [buddy]))
        arrivals.append((S.a_q, n_on, [q for q in near_q if q != buddy]))
        arrivals.append((S.a_p, n_rest * len(near_p), near_p))
        arrivals.append((S.a_rl, n_on * len(far_p), far_p))
        arrivals.append((S.a_fw, n_off, [src]))
        arrivals.append((S.a_r2, n_on * (len(far_q) - 1), [q for q in far_q if q != src]))
    else:
        arrivals.append((S.a_q, n_on * len(near_q), near_q))
        arrivals.append((S.a_p, n_rest * len(near_p), near_p))
        arrivals.append((S.a_fd, n_off, [src]))
        arrivals.append((S.a_rl, n_on * (len(far_p) - 1), [p for p in far_p if p != src]))
        arrivals.append((S.a_r2, n_on * len(far_q), far_q))

    ci = chips.index(topo.chip(core))
    pairs = [2 * ci, 2 * ci + 1, 2 * (1 - ci) + 1, 2 * (1 - ci)]
    ps = [T.xg_ps0, T.xg_ps1, T.xg_ps2, T.xg_ps3]
    s_d = [S.s_d0, S.s_d1, S.s_d2, S.s_d3]
    s_m = [S.s_m0, S.s_m1, S.s_m2, S.s_m3]
    s_c = [S.s_c0, S.s_c1, S.s_c2, S.s_c3]

    pe = g.tensor
    pe.wait_ge(S.ld_x, 16)
    pe.wait_ge(S.ld_rt, 16)
    pe.matmul(T.st_ps[:, 0:N], T.xs[:, :], T.rts[:, :], start=True, stop=True).then_inc(S.s_st, 1)
    pe.wait_ge(S.s_id, 2)
    pe.transpose(T.xt_ps[:, 0:D], T.xs[:, :], T.ident[:, :]).then_inc(S.s_xt, 1)
    pe.wait_ge(S.s_xts, 1)
    for i, h in enumerate(pairs):
        pe.wait_ge(s_d[i], 2)
        pe.matmul(ps[i][:, 0:2 * D], T.xts[:, :], T.dg[:, h * 2 * D:(h + 1) * 2 * D],
                  start=True, stop=True).then_inc(s_m[i], 1)
    seq = [(sem, cnt, c) for sem, cnt, cs in arrivals for c in cs]
    waited = []
    mm = None
    for k, (sem, cnt, c) in enumerate(seq):
        i = pairs.index(slot[c] // 2)
        if i not in waited:
            pe.wait_ge(s_c[i], 1)
            waited.append(i)
        pe.wait_ge(sem, cnt)
        mm = pe.matmul(T.y_ps[:, 0:D], W(c), T.xg[:, slot[c] * D:(slot[c] + 1) * D],
                       start=(k == 0), stop=(k == len(seq) - 1))
    mm.then_inc(S.s_y, 1)

    act = g.scalar
    for n_done, (c0, sem, cnt) in enumerate(((o0, S.s_io, 1), (b0, S.a_io, n_on))):
        act.wait_ge(sem, cnt)
        act.activation(T.sq[:, c0:c0 + H], T.pmi[:, c0:c0 + H], ActivationFunctionType.Square).then_inc(S.s_sq, 1)
        act.wait_ge(S.s_sq, n_done + 1)
        act.activation(T.ident[:, c0:c0 + H], T.sq[:, c0:c0 + H], ActivationFunctionType.Exp,
                       scale=-100.0).then_inc(S.s_id, 1)
    act.wait_ge(S.s_nm, 1)
    act.activation(T.ee[:, :], T.st_ps[:, 0:N], ActivationFunctionType.Exp, bias=T.negm[:, 0:1], scale=1.0,
                   accum_out=T.ssum[:, 0:1]).then_inc(S.s_e, 1)
    for i in (0, 2):
        h = pairs[i]
        act.wait_ge(s_m[i], 1)
        act.activation(T.xg[:, h * 2 * D:(h + 1) * 2 * D], ps[i][:, 0:2 * D],
                       ActivationFunctionType.Copy).then_inc(s_c[i], 1)

    ve = g.vector
    ve.wait_ge(S.s_st, 1)
    ve.tensor_reduce(out=T.negm[:, 0:1], in_=T.st_ps[:, 0:N], axis=AxisListType.X, op=AluOpType.max,
                     negate=True).then_inc(S.s_nm, 1)
    ve.wait_ge(S.s_e, 1)
    ve.reciprocal(T.rs[:, 0:1], T.ssum[:, 0:1]).then_inc(S.s_rs, 1)
    ve.wait_ge(S.s_xt, 1)
    ve.tensor_copy(T.xts[:, :], T.xt_ps[:, 0:D]).then_inc(S.s_xts, 1)
    ve.wait_ge(S.s_rs, 1)
    ve.wait_ge(S.s_id, 2)
    for i, h in enumerate(pairs):
        for s in (2 * h, 2 * h + 1):
            j = T.rank_of(order[s])
            ve.tensor_scalar(out=T.dg[:, s * D:(s + 1) * D], in0=T.ident[:, :], scalar1=T.ee[:, j:j + 1],
                             scalar2=T.rs[:, 0:1], op0=AluOpType.mult, op1=AluOpType.mult).then_inc(s_d[i], 1)
    for i in (1, 3):
        h = pairs[i]
        ve.wait_ge(s_m[i], 1)
        ve.tensor_copy(T.xg[:, h * 2 * D:(h + 1) * 2 * D], ps[i][:, 0:2 * D]).then_inc(s_c[i], 1)
    ve.wait_ge(S.s_y, 1)
    ve.tensor_copy(T.ysb[:, :], T.y_ps[:, 0:D]).then_inc(S.s_yc, 1)

    g.sync.wait_ge(S.s_yc, 1)
    g.sync.dma_start(T.y[:, :], T.ysb[:, :]).then_inc(S.st_y, 16)
    g.sync.wait_ge(S.st_y, 16)
